import numpy as np
import ml_dtypes


def mxq(x, axis, fmt="e4m3"):
    dtype, down = {"e4m3": (ml_dtypes.float8_e4m3fn, 7), "e5m2": (ml_dtypes.float8_e5m2, 14)}[fmt]
    v = np.moveaxis(np.asarray(x, np.float32).astype(ml_dtypes.bfloat16).astype(np.float64), axis, -1)
    blocks = v.reshape(v.shape[:-1] + (-1, 32))
    amax = np.abs(blocks).max(-1, keepdims=True)
    byte = np.maximum(np.where(amax > 0, np.frexp(amax)[1] - 1 + 127, 0) - down, 1)
    scale = np.exp2(byte - 127.0)
    codes = (blocks / scale).astype(np.float32).astype(dtype).astype(np.float64)
    return np.moveaxis((codes * scale).reshape(v.shape), -1, axis)


WIDE = False


def mx_kscale(k):
    if not WIDE:
        return np.ones(k)
    levels = np.array([10, -10, 5, -5, 0])
    if k % 512:
        return np.exp2(np.random.permutation(np.resize(levels, k // 32))).repeat(32)
    a = np.empty((k // 512, 16))
    for p in range(k // 512):
        a[p, :8] = np.random.permutation(np.resize(levels, 8))
        for g in range(8):
            far = levels[np.abs(levels - a[p, g]) >= 10]
            a[p, g + 8] = far[np.random.randint(len(far))]
    return np.exp2(a.ravel()).repeat(32)


def f64(x):
    return np.asarray(x).astype(np.float64)


def striped(idx):
    return np.tile(idx.reshape(-1, 16).T, (8, 1)).astype(np.uint16)


def unstriped(offs):
    return offs[:16].T.reshape(-1).astype(np.int64)


E2M1 = np.array([0.0, 0.5, 1.0, 1.5, 2.0, 3.0, 4.0, 6.0, -0.0, -0.5, -1.0, -1.5, -2.0, -3.0, -4.0, -6.0])


def pack_weight(w, fmt):
    k, n = w.shape
    w = f64(np.asarray(w, np.float32).astype(ml_dtypes.bfloat16)).reshape(k // 32, 32, n)
    amax = np.abs(w).max(1)
    if fmt == "e4m3":
        byte = np.frexp(amax)[1] - 1 + 127 - 7
    else:
        mant, ex = np.frexp(amax / 6.0)
        byte = np.where(mant > 0.5, ex, ex - 1) + 127
    byte = np.clip(np.where(amax > 0, byte, 1), 1, 254)
    scaled = (w * np.exp2(127.0 - byte)[:, None, :]).reshape(k, n).astype(np.float32)
    by_word = np.ascontiguousarray(scaled.reshape(k // 512, 128, 4, n).transpose(0, 1, 3, 2))
    if fmt == "e4m3":
        words = by_word.astype(ml_dtypes.float8_e4m3fn).view(np.uint8)
    else:
        c = by_word.astype(ml_dtypes.float4_e2m1fn).view(np.uint8) & 0xF
        words = (c[..., 0::2] | (c[..., 1::2] << 4)).reshape(k // 512, 128, 2 * n)
    return np.ascontiguousarray(words), np.ascontiguousarray(byte.astype(np.uint8).reshape(k // 512, 16, n))


def unpack_weight(words, scales, fmt):
    g, _, n = scales.shape
    words = np.ascontiguousarray(words).reshape(g, 128, n, -1)
    if fmt == "e4m3":
        vals = words.view(ml_dtypes.float8_e4m3fn).astype(np.float64)
    else:
        nib = np.empty((g, 128, n, 4), np.uint8)
        nib[..., 0::2] = words & 0xF
        nib[..., 1::2] = words >> 4
        vals = E2M1[nib]
    vals = vals * np.repeat(np.exp2(scales.astype(np.float64) - 127.0), 8, axis=1)[..., None]
    return vals.transpose(0, 1, 3, 2).reshape(g * 512, n)


def planes(y):
    n, m = y.shape
    v = y.astype(np.float32).astype(ml_dtypes.bfloat16).astype(np.float64).reshape(n // 32, 32, m)
    top = np.abs(v).max(1)
    byte = np.clip(np.where(top > 0, np.frexp(top)[1] - 1 + 127 - 7, 1), 1, 254)
    codes = (v * np.exp2(127.0 - byte)[:, None, :]).reshape(n, m).astype(np.float32).astype(ml_dtypes.float8_e4m3fn).view(np.uint8)
    words = codes.reshape(n // 512, 128, 4, m).transpose(0, 1, 3, 2)
    return np.ascontiguousarray(words), np.ascontiguousarray(byte.astype(np.uint8).reshape(n // 512, 16, m))


K, T, E, C, H, N = 512, 768, 6, 256, 512, 512


def by_expert(wq, xq):
    return np.concatenate([wq[e].T @ xq[:, e * C:(e + 1) * C] for e in range(E)], axis=1)


def setup_inputs():
    n = np.random.standard_normal
    s = mx_kscale(K)
    u = mx_kscale(H)
    slot_token = np.concatenate([np.random.permutation(T)[:C] for e in range(E)])
    partner = np.concatenate([np.random.permutation(T) for _ in range(-(-E * C // T))])[:E * C]
    x = pack_weight(n((K, T)) * s[:, None], "e4m3")
    w1 = [pack_weight(m, "e4m3") for m in n((E, K, H)) / np.sqrt(K) / s[None, :, None] * u]
    w2 = [pack_weight(m, "e4m3") for m in n((E, H, N)) / np.sqrt(H) / u[None, :, None]]
    return {
        "x_words": x[0],
        "x_scales": x[1],
        "w1_words": np.stack([m[0] for m in w1]),
        "w1_scales": np.stack([m[1] for m in w1]),
        "wp": (n((E, K, H)) / np.sqrt(K) / s[None, :, None] * u).astype(np.float32),
        "w2_words": np.stack([m[0] for m in w2]),
        "w2_scales": np.stack([m[1] for m in w2]),
        "offs": striped(slot_token),
        "offs2": striped(partner),
    }


def reference(x_words, x_scales, w1_words, w1_scales, wp, w2_words, w2_scales, offs, offs2):
    w1 = np.stack([unpack_weight(w1_words[e], w1_scales[e], "e4m3") for e in range(E)])
    wpq = mxq(f64(wp), 1, "e4m3")
    w2 = np.stack([unpack_weight(w2_words[e], w2_scales[e], "e4m3") for e in range(E)])
    idx, idx2 = unstriped(offs), unstriped(offs2)
    x = unpack_weight(x_words, x_scales, "e4m3")
    h = by_expert(w1, x[:, idx]) + by_expert(wpq, x[:, idx2])
    y = by_expert(w2, mxq(h, 0, "e4m3"))
    out = y
    out_0 = out
    return (out_0,) + planes(out_0)

@@ -1,0 +1,303 @@
+from contextlib import ExitStack
+
+import concourse.mybir as mybir
+
+K, T, E, C, H, N = 512, 768, 6, 256, 512, 512
+FLOPS = 2 * E * C * (2 * K * H + H * N)
+
+F32 = mybir.dt.float32
+BF16 = mybir.dt.bfloat16
+I32 = mybir.dt.int32
+U32 = mybir.dt.uint32
+U16 = mybir.dt.uint16
+U8 = mybir.dt.uint8
+FP8X4 = mybir.dt.float8_e4m3fn_x4
+
+P = 128
+PACK = 4
+HALF = 128
+QUADS = 4
+WP_LAST = 1
+
+
+def tile_moe_duo_s_none_kernel(
+    tc, x_words, x_scales, w1_words, w1_scales, wp, w2_words, w2_scales, offs, offs2, out_0, out_1, out_2
+):
+    nc = tc.nc
+    with ExitStack() as ctx:
+        keep = ctx.enter_context(tc.tile_pool(name="keep", bufs=1))
+        ring = ctx.enter_context(tc.tile_pool(name="ring", bufs=3))
+        psum = ctx.enter_context(tc.psum_pool(name="psum", bufs=4))
+
+        tok_list = keep.tile([P, E * C // 16], U16, name="tok_list")
+        par_list = keep.tile([P, E * C // 16], U16, name="par_list")
+        x_w = keep.tile([P, T], I32, name="x_w", align_bytes=64)
+        x_s = keep.tile([P, T], U8, name="x_s", align_bytes=64)
+        s_raw = [keep.tile([P, H], U8, name=f"s_raw{g}", align_bytes=64) for g in range(3)]
+        s_dealt = [keep.tile([P, H], U8, name=f"s_dealt{g}", align_bytes=64) for g in range(3)]
+        y_s = keep.tile([P, E * C], U8, name="y_s", align_bytes=64)
+
+        nc.vector.memset(x_s[:].bitcast(I32), 0)
+        for g in range(3):
+            nc.vector.memset(s_raw[g][:].bitcast(I32), 0)
+
+        w_scales = (w1_scales.bitcast(I32), w2_scales.bitcast(I32))
+        w_words = (w1_words, w2_words)
+
+        def load_scales(m, late):
+            for q in range(QUADS):
+                if late:
+                    dst = s_raw[2][:].bitcast(I32)[32 * q + 8 * m : 32 * q + 8 * m + 8, :]
+                    nc.sync.dma_start(out=dst, in_=w_scales[m][4:6, 0, 4 * q : 4 * q + 4, :])
+                else:
+                    dst = s_raw[m][:].bitcast(I32)[32 * q : 32 * q + 16, :]
+                    nc.sync.dma_start(out=dst, in_=w_scales[m][0:4, 0, 4 * q : 4 * q + 4, :])
+
+        def plane(m, e):
+            g, a = (m, e) if e < 4 else (2, 2 * m + e - 4)
+            return s_dealt[g][4 * a : P, :]
+
+        wp_raw = {}
+        w_raw = {}
+
+        def load_wp(e):
+            src = wp[e].rearrange("(p j) i -> p j i", j=PACK)
+            if e == 0:
+                for h in range(2):
+                    t = keep.tile([P, PACK, H // 2], F32, name=f"wp_raw{e}_{h}")
+                    nc.sync.dma_start(out=t[:], in_=src[:, :, h * (H // 2) : (h + 1) * (H // 2)])
+                    wp_raw[e, h] = t[:]
+            else:
+                t = keep.tile([P, PACK, H], F32, name=f"wp_raw{e}", tag=f"stage{e}", align_bytes=64)
+                nc.sync.dma_start(out=t[:], in_=src)
+                wp_raw[e, 0] = t[:]
+
+        def load_w(m, e):
+            t = keep.tile([P, H], I32, name=f"w_raw{m}_{e}")
+            nc.sync.dma_start(out=t[:], in_=w_words[m][e, 0].rearrange("p n t -> p (n t)").bitcast(I32))
+            w_raw[m, e] = t
+
+        nc.sync.dma_start(tok_list[:], offs)
+        nc.sync.dma_start(out=x_w[:], in_=x_words[0].rearrange("p n t -> p (n t)").bitcast(I32))
+        load_wp(0)
+        nc.sync.dma_start(par_list[:], offs2)
+        load_wp(1)
+        for q in range(QUADS):
+            nc.sync.dma_start(
+                out=x_s[:].bitcast(I32)[32 * q : 32 * q + 4, :], in_=x_scales.bitcast(I32)[0, 4 * q : 4 * q + 4, :]
+            )
+        for e in range(2, E - 1):
+            load_wp(e)
+            if e < 4:
+                load_scales(e % 2, False)
+                load_w(0, e - 2)
+        for e in range(E):
+            if e == WP_LAST:
+                load_wp(E - 1)
+            load_w(1, e)
+            if e + 2 < E:
+                load_w(0, e + 2)
+            if e < 2:
+                load_scales(e, True)
+
+        gathered = {}
+        wp_bf = {}
+        wp_q = {}
+        w_dealt = {}
+        h_bf = {}
+        h_q = {}
+        y_f = {}
+        y_bf = {}
+        h_ps = {}
+        y_ps = {}
+
+        def gather(window, dtype, nm):
+            for g in range(E // 2):
+                cols = slice(g * 2 * C // 16, (g + 1) * 2 * C // 16)
+                for lnm, lst in (("tok", tok_list), ("par", par_list)):
+                    t = keep.tile([P, 2 * C], dtype, name=f"{lnm}_{nm}{g}", align_bytes=64)
+                    nc.vector.tensor_copy(t[:], window.indirect(lst[:, cols]))
+                    for i in range(2):
+                        gathered[lnm, nm, 2 * g + i] = t[:, i * C : (i + 1) * C]
+
+        def deal_scales(g):
+            nc.vector.tensor_copy(
+                out=s_dealt[g][:].rearrange("p (t m) -> p t m", t=PACK), in_=s_raw[g][:].rearrange("p (m t) -> p t m", t=PACK)
+            )
+
+        def deal_words(m, e):
+            t = keep.tile([P, PACK, P], I32, name=f"w_dealt{m}_{e}", align_bytes=64)
+            if m == 0 and e < 2:
+                nc.scalar.copy(
+                    out=t[:].bitcast(U32).rearrange("p t m -> p m t"),
+                    in_=w_raw[m, e][:].bitcast(U32).rearrange("p (m t) -> p m t", t=PACK),
+                )
+            else:
+                nc.vector.tensor_copy(
+                    out=t[:].rearrange("p t m -> p m t"), in_=w_raw[m, e][:].rearrange("p (m t) -> p m t", t=PACK)
+                )
+            w_dealt[m, e] = t
+
+        def round_wp(e):
+            t = keep.tile([P, PACK, P, PACK], BF16, name=f"wp_bf{e}", align_bytes=64)
+            parts = 2 if e == 0 else 1
+            for h in range(parts):
+                cp = nc.vector.tensor_copy if e == E - 1 else nc.scalar.copy
+                cp(
+                    out=t[:, :, h * P // parts : (h + 1) * P // parts, :].rearrange("p t m j -> p m j t"),
+                    in_=wp_raw[e, h].rearrange("p j (m t) -> p m j t", t=PACK),
+                )
+            wp_bf[e] = t
+
+        def quant_wp(e):
+            w = keep.tile([P, H], U32, name=f"wp_w{e}", align_bytes=64)
+            s = keep.tile([P, H], U8, name=f"wp_s{e}", align_bytes=64)
+            nc.vector.quantize_mx(out=w[:].bitcast(FP8X4), scales=s[:], in_=wp_bf[e][:].rearrange("p t m j -> p (t m j)"))
+            wp_q[e] = (w, s)
+
+        def layer1(e):
+            tok_w, par_w, tok_s, par_s = (gathered[a, b, e] for b in ("w", "s") for a in ("tok", "par"))
+            for h in range(2):
+                cols = slice(h * HALF, (h + 1) * HALF)
+                ps = psum.tile([P, PACK, HALF], F32, name="h_ps")
+                for t in range(PACK):
+                    ch = slice(t * P, (t + 1) * P)
+                    nc.tensor.matmul_mx(
+                        out=ps[:, t, :],
+                        lhsT=w_dealt[0, e][:, t, :].bitcast(FP8X4),
+                        lhsT_scale=plane(0, e)[:, ch],
+                        rhs=tok_w[:, cols].bitcast(FP8X4),
+                        rhs_scale=tok_s[:, cols],
+                        start=True,
+                        stop=False,
+                    )
+                    nc.tensor.matmul_mx(
+                        out=ps[:, t, :],
+                        lhsT=wp_q[e][0][:, ch].bitcast(FP8X4),
+                        lhsT_scale=wp_q[e][1][:, ch],
+                        rhs=par_w[:, cols].bitcast(FP8X4),
+                        rhs_scale=par_s[:, cols],
+                        start=False,
+                        stop=True,
+                    )
+                h_ps[e, h] = ps
+
+        def round_h(e):
+            if e == 0:
+                first = keep.tile([P, 2, C, PACK], BF16, name="h_bf01", tag=f"stage{E - 2}", align_bytes=64)
+                h_bf[0], h_bf[1] = first[:, 0], first[:, 1]
+            if e > 1:
+                h_bf[e] = ring.tile([P, C, PACK], BF16, name="h_bf", align_bytes=64)
+            t = h_bf[e]
+            for h in range(2):
+                nc.scalar.copy(out=t[:, h * HALF : (h + 1) * HALF, :], in_=h_ps[e, h][:].rearrange("p t n -> p n t"))
+
+        def quant_h(e):
+            w = ring.tile([P, C], U32, name="h_w", align_bytes=64)
+            s = ring.tile([P, C], U8, name="h_s", align_bytes=64)
+            nc.vector.quantize_mx(out=w[:].bitcast(FP8X4), scales=s[:], in_=h_bf[e][:].rearrange("p n t -> p (n t)"))
+            h_q[e] = (w, s)
+
+        def last_expert(e):
+            banks = []
+            for h in range(2):
+                cols = slice(h * HALF, (h + 1) * HALF)
+                ps = psum.tile([P, PACK, HALF], F32, name="y_ps")
+                for t in range(PACK):
+                    nc.tensor.matmul_mx(
+                        out=ps[:, t, :],
+                        lhsT=w_dealt[1, e][:, t, :].bitcast(FP8X4),
+                        lhsT_scale=plane(1, e)[:, t * P : (t + 1) * P],
+                        rhs=h_q[e][0][:, cols].bitcast(FP8X4),
+                        rhs_scale=h_q[e][1][:, cols],
+                        start=True,
+                        stop=True,
+                    )
+                banks.append(ps)
+            yb = ring.tile([P, C, PACK], BF16, name="y_bf", align_bytes=64)
+            for h in range(2):
+                cols = slice(h * HALF, (h + 1) * HALF)
+                yf = keep.tile([P, PACK, HALF], F32, name=f"y_f{e}_{h}")
+                nc.scalar.copy(out=yf[:], in_=banks[h][:])
+                nc.sync.dma_start(
+                    out=out_0.rearrange("(p t) j -> p t j", t=PACK)[:, :, e * C + h * HALF : e * C + (h + 1) * HALF],
+                    in_=yf[:],
+                )
+                nc.vector.tensor_copy(
+                    out=yb[:, cols, :].rearrange("p (c i) t -> p c t i", i=4),
+                    in_=yf[:].rearrange("p t (c i) -> p c t i", i=4),
+                )
+            y_bf[e] = yb
+
+        def layer2(e):
+            for b in range(2):
+                ps = psum.tile([P, 2, C], F32, name="y_ps")
+                for i in range(2):
+                    t = 2 * b + i
+                    nc.tensor.matmul_mx(
+                        out=ps[:, i, :],
+                        lhsT=w_dealt[1, e][:, t, :].bitcast(FP8X4),
+                        lhsT_scale=plane(1, e)[:, t * P : (t + 1) * P],
+                        rhs=h_q[e][0][:].bitcast(FP8X4),
+                        rhs_scale=h_q[e][1][:],
+                        start=True,
+                        stop=True,
+                    )
+                y_ps[e, b] = ps
+
+        def copy_y(e):
+            t = keep.tile([P, PACK, C], F32, name=f"y_f{e}")
+            for b in range(2):
+                nc.scalar.copy(out=t[:, 2 * b : 2 * b + 2, :], in_=y_ps[e, b][:])
+            y_f[e] = t
+            nc.sync.dma_start(out=out_0.rearrange("(p t) j -> p t j", t=PACK)[:, :, e * C : (e + 1) * C], in_=t[:])
+
+        def round_y(e):
+            t = ring.tile([P, C, PACK], BF16, name="y_bf", align_bytes=64)
+            nc.vector.tensor_copy(
+                out=t[:].rearrange("p (c i) t -> p c t i", i=4), in_=y_f[e][:].rearrange("p t (c i) -> p c t i", i=4)
+            )
+            y_bf[e] = t
+
+        def quant_y(e):
+            w = keep.tile([P, C], U32, name=f"y_w{e}", align_bytes=64)
+            nc.vector.quantize_mx(
+                out=w[:].bitcast(FP8X4), scales=y_s[:, e * C : (e + 1) * C], in_=y_bf[e][:].rearrange("p n t -> p (n t)")
+            )
+            nc.sync.dma_start(
+                out=out_1[0].rearrange("p n t -> p (n t)").bitcast(I32)[:, e * C : (e + 1) * C], in_=w[:].bitcast(I32)
+            )
+
+        gather(x_w[:].bitcast(U32), U32, "w")
+        gather(x_s[:], U8, "s")
+        for e in range(E - 1):
+            round_wp(e)
+            if e in (2, 3):
+                deal_words(0, e - 2)
+        for g in range(3):
+            deal_scales(g)
+        for e in range(E + 2):
+            if e == E - 1:
+                round_wp(e)
+            if e < E:
+                quant_wp(e)
+                if e >= 2:
+                    deal_words(0, e)
+                layer1(e)
+                round_h(e)
+                deal_words(1, e)
+            if 1 <= e <= E:
+                quant_h(e - 1)
+                if e < E:
+                    layer2(e - 1)
+                    copy_y(e - 1)
+                else:
+                    last_expert(e - 1)
+            if e >= 2:
+                if e - 2 < E - 1:
+                    round_y(e - 2)
+                quant_y(e - 2)
+        for q in range(QUADS):
+            nc.sync.dma_start(
+                out=out_2.bitcast(I32)[0, 4 * q : 4 * q + 4, :], in_=y_s[:].bitcast(I32)[32 * q : 32 * q + 4, :]
+            )

@@ -17,7 +17,6 @@ P = 128
 PACK = 4
 HALF = 128
 QUADS = 4
-WP_LAST = 1
 
 
 def tile_moe_duo_s_none_kernel(
@@ -86,19 +85,15 @@ def tile_moe_duo_s_none_kernel(
             nc.sync.dma_start(
                 out=x_s[:].bitcast(I32)[32 * q : 32 * q + 4, :], in_=x_scales.bitcast(I32)[0, 4 * q : 4 * q + 4, :]
             )
-        for e in range(2, E - 1):
+        for e in range(2, E):
             load_wp(e)
-            if e < 4:
-                load_scales(e % 2, False)
-                load_w(0, e - 2)
+            load_scales(e % 2, e >= 4)
+            if e == 2:
+                load_w(0, 0)
         for e in range(E):
-            if e == WP_LAST:
-                load_wp(E - 1)
+            if e + 1 < E:
+                load_w(0, e + 1)
             load_w(1, e)
-            if e + 2 < E:
-                load_w(0, e + 2)
-            if e < 2:
-                load_scales(e, True)
 
         gathered = {}
         wp_bf = {}
@@ -127,25 +122,16 @@ def tile_moe_duo_s_none_kernel(
 
         def deal_words(m, e):
             t = keep.tile([P, PACK, P], I32, name=f"w_dealt{m}_{e}", align_bytes=64)
-            if m == 0 and e < 2:
-                nc.scalar.copy(
-                    out=t[:].bitcast(U32).rearrange("p t m -> p m t"),
-                    in_=w_raw[m, e][:].bitcast(U32).rearrange("p (m t) -> p m t", t=PACK),
-                )
-            else:
-                nc.vector.tensor_copy(
-                    out=t[:].rearrange("p t m -> p m t"), in_=w_raw[m, e][:].rearrange("p (m t) -> p m t", t=PACK)
-                )
+            nc.vector.tensor_copy(out=t[:].rearrange("p t m -> p m t"), in_=w_raw[m, e][:].rearrange("p (m t) -> p m t", t=PACK))
             w_dealt[m, e] = t
 
         def round_wp(e):
             t = keep.tile([P, PACK, P, PACK], BF16, name=f"wp_bf{e}", align_bytes=64)
             parts = 2 if e == 0 else 1
             for h in range(parts):
-                cp = nc.vector.tensor_copy if e == E - 1 else nc.scalar.copy
-                cp(
-                    out=t[:, :, h * P // parts : (h + 1) * P // parts, :].rearrange("p t m j -> p m j t"),
-                    in_=wp_raw[e, h].rearrange("p j (m t) -> p m j t", t=PACK),
+                nc.scalar.copy(
+                    out=t[:, :, h * P // parts : (h + 1) * P // parts, :].rearrange("p t (m u) j -> p m j t u", u=2),
+                    in_=wp_raw[e, h].rearrange("p j (m u t) -> p m j t u", u=2, t=PACK),
                 )
             wp_bf[e] = t
 
@@ -184,13 +170,14 @@ def tile_moe_duo_s_none_kernel(
 
         def round_h(e):
             if e == 0:
-                first = keep.tile([P, 2, C, PACK], BF16, name="h_bf01", tag=f"stage{E - 2}", align_bytes=64)
+                first = keep.tile([P, 2, C, PACK], BF16, name="h_bf01", tag=f"stage{E - 1}", align_bytes=64)
                 h_bf[0], h_bf[1] = first[:, 0], first[:, 1]
             if e > 1:
                 h_bf[e] = ring.tile([P, C, PACK], BF16, name="h_bf", align_bytes=64)
             t = h_bf[e]
             for h in range(2):
-                nc.scalar.copy(out=t[:, h * HALF : (h + 1) * HALF, :], in_=h_ps[e, h][:].rearrange("p t n -> p n t"))
+                cp = nc.vector.tensor_copy if (e == E - 1 and h == 1) else nc.scalar.copy
+                cp(out=t[:, h * HALF : (h + 1) * HALF, :], in_=h_ps[e, h][:].rearrange("p t n -> p n t"))
 
         def quant_h(e):
             w = ring.tile([P, C], U32, name="h_w", align_bytes=64)
@@ -214,19 +201,13 @@ def tile_moe_duo_s_none_kernel(
                         stop=True,
                     )
                 banks.append(ps)
+            yf = keep.tile([P, PACK, C], F32, name=f"y_f{e}")
             yb = ring.tile([P, C, PACK], BF16, name="y_bf", align_bytes=64)
-            for h in range(2):
-                cols = slice(h * HALF, (h + 1) * HALF)
-                yf = keep.tile([P, PACK, HALF], F32, name=f"y_f{e}_{h}")
-                nc.scalar.copy(out=yf[:], in_=banks[h][:])
-                nc.sync.dma_start(
-                    out=out_0.rearrange("(p t) j -> p t j", t=PACK)[:, :, e * C + h * HALF : e * C + (h + 1) * HALF],
-                    in_=yf[:],
-                )
-                nc.vector.tensor_copy(
-                    out=yb[:, cols, :].rearrange("p (c i) t -> p c t i", i=4),
-                    in_=yf[:].rearrange("p t (c i) -> p c t i", i=4),
-                )
+            nc.scalar.copy(out=yf[:, :, 0:HALF], in_=banks[0][:])
+            nc.vector.tensor_copy(out=yb[:, HALF:C, :], in_=banks[1][:].rearrange("p t n -> p n t"))
+            nc.vector.tensor_copy(out=yb[:, 0:HALF, :], in_=banks[0][:].rearrange("p t n -> p n t"))
+            nc.scalar.copy(out=yf[:, :, HALF:C], in_=banks[1][:])
+            nc.sync.dma_start(out=out_0.rearrange("(p t) j -> p t j", t=PACK)[:, :, e * C : (e + 1) * C], in_=yf[:])
             y_bf[e] = yb
 
         def layer2(e):
@@ -270,19 +251,14 @@ def tile_moe_duo_s_none_kernel(
 
         gather(x_w[:].bitcast(U32), U32, "w")
         gather(x_s[:], U8, "s")
-        for e in range(E - 1):
+        for e in range(E):
             round_wp(e)
-            if e in (2, 3):
-                deal_words(0, e - 2)
         for g in range(3):
             deal_scales(g)
         for e in range(E + 2):
-            if e == E - 1:
-                round_wp(e)
             if e < E:
                 quant_wp(e)
-                if e >= 2:
-                    deal_words(0, e)
+                deal_words(0, e)
                 layer1(e)
                 round_h(e)
                 deal_words(1, e)

@@ -36,9 +36,9 @@ def tile_moe_duo_s_none_kernel(
         s_dealt = [keep.tile([P, H], U8, name=f"s_dealt{g}", align_bytes=64) for g in range(3)]
         y_s = keep.tile([P, E * C], U8, name="y_s", align_bytes=64)
 
-        nc.vector.memset(x_s[:].bitcast(I32), 0)
+        nc.gpsimd.memset(x_s[:].bitcast(I32), 0)
         for g in range(3):
-            nc.vector.memset(s_raw[g][:].bitcast(I32), 0)
+            nc.gpsimd.memset(s_raw[g][:].bitcast(I32), 0)
 
         w_scales = (w1_scales.bitcast(I32), w2_scales.bitcast(I32))
         w_words = (w1_words, w2_words)
@@ -87,9 +87,12 @@ def tile_moe_duo_s_none_kernel(
             )
         for e in range(2, E):
             load_wp(e)
-            load_scales(e % 2, e >= 4)
             if e == 2:
+                load_scales(0, False)
                 load_w(0, 0)
+                load_scales(1, False)
+            elif e < 5:
+                load_scales(e - 3, True)
         for e in range(E):
             if e + 1 < E:
                 load_w(0, e + 1)
@@ -116,13 +119,18 @@ def tile_moe_duo_s_none_kernel(
                         gathered[lnm, nm, 2 * g + i] = t[:, i * C : (i + 1) * C]
 
         def deal_scales(g):
-            nc.vector.tensor_copy(
+            nc.gpsimd.tensor_copy(
                 out=s_dealt[g][:].rearrange("p (t m) -> p t m", t=PACK), in_=s_raw[g][:].rearrange("p (m t) -> p t m", t=PACK)
             )
 
         def deal_words(m, e):
             t = keep.tile([P, PACK, P], I32, name=f"w_dealt{m}_{e}", align_bytes=64)
-            nc.vector.tensor_copy(out=t[:].rearrange("p t m -> p m t"), in_=w_raw[m, e][:].rearrange("p (m t) -> p m t", t=PACK))
+            if (m, e) == (0, 0):
+                nc.gpsimd.tensor_copy(out=t[:], in_=w_raw[m, e][:].rearrange("p (m t) -> p t m", t=PACK))
+            else:
+                nc.vector.tensor_copy(
+                    out=t[:].rearrange("p t m -> p m t"), in_=w_raw[m, e][:].rearrange("p (m t) -> p m t", t=PACK)
+                )
             w_dealt[m, e] = t
 
         def round_wp(e):
@@ -201,13 +209,19 @@ def tile_moe_duo_s_none_kernel(
                         stop=True,
                     )
                 banks.append(ps)
-            yf = keep.tile([P, PACK, C], F32, name=f"y_f{e}")
             yb = ring.tile([P, C, PACK], BF16, name="y_bf", align_bytes=64)
-            nc.scalar.copy(out=yf[:, :, 0:HALF], in_=banks[0][:])
-            nc.vector.tensor_copy(out=yb[:, HALF:C, :], in_=banks[1][:].rearrange("p t n -> p n t"))
-            nc.vector.tensor_copy(out=yb[:, 0:HALF, :], in_=banks[0][:].rearrange("p t n -> p n t"))
-            nc.scalar.copy(out=yf[:, :, HALF:C], in_=banks[1][:])
-            nc.sync.dma_start(out=out_0.rearrange("(p t) j -> p t j", t=PACK)[:, :, e * C : (e + 1) * C], in_=yf[:])
+            for h in range(2):
+                cols = slice(h * HALF, (h + 1) * HALF)
+                yf = keep.tile([P, PACK, HALF], F32, name=f"y_f{e}_{h}")
+                nc.scalar.copy(out=yf[:], in_=banks[h][:])
+                nc.sync.dma_start(
+                    out=out_0.rearrange("(p t) j -> p t j", t=PACK)[:, :, e * C + h * HALF : e * C + (h + 1) * HALF],
+                    in_=yf[:],
+                )
+                nc.vector.tensor_copy(
+                    out=yb[:, cols, :].rearrange("p (c i) t -> p c t i", i=4),
+                    in_=yf[:].rearrange("p t (c i) -> p c t i", i=4),
+                )
             y_bf[e] = yb
 
         def layer2(e):

@@ -71,10 +71,11 @@ def tile_moe_duo_s_none_kernel(
                 nc.sync.dma_start(out=t[:], in_=src)
                 wp_raw[e, 0] = t[:]
 
-        def load_w(m, e):
-            t = keep.tile([P, H], I32, name=f"w_raw{m}_{e}")
-            nc.sync.dma_start(out=t[:], in_=w_words[m][e, 0].rearrange("p n t -> p (n t)").bitcast(I32))
-            w_raw[m, e] = t
+        def load_w(m, e, n):
+            t = keep.tile([P, n, H], I32, name=f"w_raw{m}_{e}")
+            nc.sync.dma_start(out=t[:], in_=w_words[m][e : e + n, 0].rearrange("e p n t -> p e (n t)").bitcast(I32))
+            for i in range(n):
+                w_raw[m, e + i] = t[:, i, :]
 
         nc.sync.dma_start(tok_list[:], offs)
         nc.sync.dma_start(out=x_w[:], in_=x_words[0].rearrange("p n t -> p (n t)").bitcast(I32))
@@ -89,14 +90,15 @@ def tile_moe_duo_s_none_kernel(
             load_wp(e)
             if e == 2:
                 load_scales(0, False)
-                load_w(0, 0)
+                load_w(0, 0, 1)
                 load_scales(1, False)
             elif e < 5:
                 load_scales(e - 3, True)
-        for e in range(E):
-            if e + 1 < E:
-                load_w(0, e + 1)
-            load_w(1, e)
+        load_w(0, 1, 1)
+        for e in range(0, E, 2):
+            load_w(1, e, 2)
+            if e + 2 < E:
+                load_w(0, e + 2, 2)
 
         gathered = {}
         wp_bf = {}
@@ -105,6 +107,7 @@ def tile_moe_duo_s_none_kernel(
         h_bf = {}
         h_q = {}
         y_f = {}
+        y_pair = {}
         y_bf = {}
         h_ps = {}
         y_ps = {}
@@ -126,10 +129,11 @@ def tile_moe_duo_s_none_kernel(
         def deal_words(m, e):
             t = keep.tile([P, PACK, P], I32, name=f"w_dealt{m}_{e}", align_bytes=64)
             if (m, e) == (0, 0):
-                nc.gpsimd.tensor_copy(out=t[:], in_=w_raw[m, e][:].rearrange("p (m t) -> p t m", t=PACK))
+                nc.gpsimd.tensor_copy(out=t[:], in_=w_raw[m, e].rearrange("p (m t) -> p t m", t=PACK))
             else:
                 nc.vector.tensor_copy(
-                    out=t[:].rearrange("p t m -> p m t"), in_=w_raw[m, e][:].rearrange("p (m t) -> p m t", t=PACK)
+                    out=t[:].rearrange("p (g t) m -> p g m t", t=2),
+                    in_=w_raw[m, e].rearrange("p (m g t) -> p g m t", g=2, t=2),
                 )
             w_dealt[m, e] = t
 
@@ -137,10 +141,10 @@ def tile_moe_duo_s_none_kernel(
             t = keep.tile([P, PACK, P, PACK], BF16, name=f"wp_bf{e}", align_bytes=64)
             parts = 2 if e == 0 else 1
             for h in range(parts):
-                nc.scalar.copy(
-                    out=t[:, :, h * P // parts : (h + 1) * P // parts, :].rearrange("p t (m u) j -> p m j t u", u=2),
-                    in_=wp_raw[e, h].rearrange("p j (m u t) -> p m j t u", u=2, t=PACK),
-                )
+                dst = t[:, :, h * P // parts : (h + 1) * P // parts, :].rearrange("p (g t) (m u) j -> p g m j u t", t=2, u=2)
+                src = wp_raw[e, h].rearrange("p j (m u g t) -> p g m j u t", u=2, g=2, t=2)
+                for g in range(2):
+                    nc.scalar.copy(out=dst[:, g], in_=src[:, g])
             wp_bf[e] = t
 
         def quant_wp(e):
@@ -255,13 +259,18 @@ def tile_moe_duo_s_none_kernel(
             y_bf[e] = t
 
         def quant_y(e):
-            w = keep.tile([P, C], U32, name=f"y_w{e}", align_bytes=64)
+            if e % 2 == 0:
+                y_pair[1] = keep.tile([P, 2 * C], U32, name=f"y_w{e}", align_bytes=64)
+            w = y_pair[1]
             nc.vector.quantize_mx(
-                out=w[:].bitcast(FP8X4), scales=y_s[:, e * C : (e + 1) * C], in_=y_bf[e][:].rearrange("p n t -> p (n t)")
+                out=w[:, (e % 2) * C : (e % 2 + 1) * C].bitcast(FP8X4),
+                scales=y_s[:, e * C : (e + 1) * C],
+                in_=y_bf[e][:].rearrange("p n t -> p (n t)"),
             )
-            nc.sync.dma_start(
-                out=out_1[0].rearrange("p n t -> p (n t)").bitcast(I32)[:, e * C : (e + 1) * C], in_=w[:].bitcast(I32)
-            )
+            if e % 2 == 1:
+                nc.sync.dma_start(
+                    out=out_1[0].rearrange("p n t -> p (n t)").bitcast(I32)[:, (e - 1) * C : (e + 1) * C], in_=w[:].bitcast(I32)
+                )
 
         gather(x_w[:].bitcast(U32), U32, "w")
         gather(x_s[:], U8, "s")

from contextlib import ExitStack

import concourse.mybir as mybir

K, T, E, C, H, N = 512, 768, 6, 256, 512, 512
FLOPS = 2 * E * C * (2 * K * H + H * N)

F32 = mybir.dt.float32
BF16 = mybir.dt.bfloat16
I32 = mybir.dt.int32
U32 = mybir.dt.uint32
U16 = mybir.dt.uint16
U8 = mybir.dt.uint8
FP8X4 = mybir.dt.float8_e4m3fn_x4

P = 128
PACK = 4
HALF = 128
QUADS = 4


def tile_moe_duo_s_none_kernel(
    tc, x_words, x_scales, w1_words, w1_scales, wp, w2_words, w2_scales, offs, offs2, out_0, out_1, out_2
):
    nc = tc.nc
    with ExitStack() as ctx:
        keep = ctx.enter_context(tc.tile_pool(name="keep", bufs=1))
        ring = ctx.enter_context(tc.tile_pool(name="ring", bufs=3))
        psum = ctx.enter_context(tc.psum_pool(name="psum", bufs=4))

        tok_list = keep.tile([P, E * C // 16], U16, name="tok_list")
        par_list = keep.tile([P, E * C // 16], U16, name="par_list")
        x_w = keep.tile([P, T], I32, name="x_w", align_bytes=64)
        x_s = keep.tile([P, T], U8, name="x_s", align_bytes=64)
        s_raw = [keep.tile([P, H], U8, name=f"s_raw{g}", align_bytes=64) for g in range(3)]
        s_dealt = [keep.tile([P, H], U8, name=f"s_dealt{g}", align_bytes=64) for g in range(3)]
        y_s = keep.tile([P, E * C], U8, name="y_s", align_bytes=64)

        nc.gpsimd.memset(x_s[:].bitcast(I32), 0)
        for g in range(3):
            nc.gpsimd.memset(s_raw[g][:].bitcast(I32), 0)

        w_scales = (w1_scales.bitcast(I32), w2_scales.bitcast(I32))
        w_words = (w1_words, w2_words)

        def load_scales(m, late):
            for q in range(QUADS):
                if late:
                    dst = s_raw[2][:].bitcast(I32)[32 * q + 8 * m : 32 * q + 8 * m + 8, :]
                    nc.sync.dma_start(out=dst, in_=w_scales[m][4:6, 0, 4 * q : 4 * q + 4, :])
                else:
                    dst = s_raw[m][:].bitcast(I32)[32 * q : 32 * q + 16, :]
                    nc.sync.dma_start(out=dst, in_=w_scales[m][0:4, 0, 4 * q : 4 * q + 4, :])

        def plane(m, e):
            g, a = (m, e) if e < 4 else (2, 2 * m + e - 4)
            return s_dealt[g][4 * a : P, :]

        wp_raw = {}
        w_raw = {}

        def load_wp(e):
            src = wp[e].rearrange("(p j) i -> p j i", j=PACK)
            if e == 0:
                for h in range(2):
                    t = keep.tile([P, PACK, H // 2], F32, name=f"wp_raw{e}_{h}")
                    nc.sync.dma_start(out=t[:], in_=src[:, :, h * (H // 2) : (h + 1) * (H // 2)])
                    wp_raw[e, h] = t[:]
            else:
                t = keep.tile([P, PACK, H], F32, name=f"wp_raw{e}", tag=f"stage{e}", align_bytes=64)
                nc.sync.dma_start(out=t[:], in_=src)
                wp_raw[e, 0] = t[:]

        def load_w(m, e, n):
            t = keep.tile([P, n, H], I32, name=f"w_raw{m}_{e}")
            nc.sync.dma_start(out=t[:], in_=w_words[m][e : e + n, 0].rearrange("e p n t -> p e (n t)").bitcast(I32))
            for i in range(n):
                w_raw[m, e + i] = t[:, i, :]

        nc.sync.dma_start(tok_list[:], offs)
        nc.sync.dma_start(out=x_w[:], in_=x_words[0].rearrange("p n t -> p (n t)").bitcast(I32))
        load_wp(0)
        nc.sync.dma_start(par_list[:], offs2)
        load_wp(1)
        for q in range(QUADS):
            nc.sync.dma_start(
                out=x_s[:].bitcast(I32)[32 * q : 32 * q + 4, :], in_=x_scales.bitcast(I32)[0, 4 * q : 4 * q + 4, :]
            )
        for e in range(2, E):
            load_wp(e)
            if e == 2:
                load_scales(0, False)
                load_w(0, 0, 1)
                load_scales(1, False)
            elif e < 5:
                load_scales(e - 3, True)
        load_w(0, 1, 1)
        for e in range(0, E, 2):
            load_w(1, e, 2)
            if e + 2 < E:
                load_w(0, e + 2, 2)

        gathered = {}
        wp_bf = {}
        wp_q = {}
        w_dealt = {}
        h_bf = {}
        h_q = {}
        y_f = {}
        y_pair = {}
        y_bf = {}
        h_ps = {}
        y_ps = {}

        def gather(window, dtype, nm):
            for g in range(E // 2):
                cols = slice(g * 2 * C // 16, (g + 1) * 2 * C // 16)
                for lnm, lst in (("tok", tok_list), ("par", par_list)):
                    t = keep.tile([P, 2 * C], dtype, name=f"{lnm}_{nm}{g}", align_bytes=64)
                    nc.vector.tensor_copy(t[:], window.indirect(lst[:, cols]))
                    for i in range(2):
                        gathered[lnm, nm, 2 * g + i] = t[:, i * C : (i + 1) * C]

        def deal_scales(g):
            nc.gpsimd.tensor_copy(
                out=s_dealt[g][:].rearrange("p (t m) -> p t m", t=PACK), in_=s_raw[g][:].rearrange("p (m t) -> p t m", t=PACK)
            )

        def deal_words(m, e):
            t = keep.tile([P, PACK, P], I32, name=f"w_dealt{m}_{e}", align_bytes=64)
            if (m, e) == (0, 0):
                nc.gpsimd.tensor_copy(out=t[:], in_=w_raw[m, e].rearrange("p (m t) -> p t m", t=PACK))
            else:
                nc.vector.tensor_copy(
                    out=t[:].rearrange("p (g t) m -> p g m t", t=2),
                    in_=w_raw[m, e].rearrange("p (m g t) -> p g m t", g=2, t=2),
                )
            w_dealt[m, e] = t

        def round_wp(e):
            t = keep.tile([P, PACK, P, PACK], BF16, name=f"wp_bf{e}", align_bytes=64)
            parts = 2 if e == 0 else 1
            for h in range(parts):
                dst = t[:, :, h * P // parts : (h + 1) * P // parts, :].rearrange("p (g t) (m u) j -> p g m j u t", t=2, u=2)
                src = wp_raw[e, h].rearrange("p j (m u g t) -> p g m j u t", u=2, g=2, t=2)
                for g in range(2):
                    nc.scalar.copy(out=dst[:, g], in_=src[:, g])
            wp_bf[e] = t

        def quant_wp(e):
            w = keep.tile([P, H], U32, name=f"wp_w{e}", align_bytes=64)
            s = keep.tile([P, H], U8, name=f"wp_s{e}", align_bytes=64)
            nc.vector.quantize_mx(out=w[:].bitcast(FP8X4), scales=s[:], in_=wp_bf[e][:].rearrange("p t m j -> p (t m j)"))
            wp_q[e] = (w, s)

        def layer1(e):
            tok_w, par_w, tok_s, par_s = (gathered[a, b, e] for b in ("w", "s") for a in ("tok", "par"))
            for h in range(2):
                cols = slice(h * HALF, (h + 1) * HALF)
                ps = psum.tile([P, PACK, HALF], F32, name="h_ps")
                for t in range(PACK):
                    ch = slice(t * P, (t + 1) * P)
                    nc.tensor.matmul_mx(
                        out=ps[:, t, :],
                        lhsT=w_dealt[0, e][:, t, :].bitcast(FP8X4),
                        lhsT_scale=plane(0, e)[:, ch],
                        rhs=tok_w[:, cols].bitcast(FP8X4),
                        rhs_scale=tok_s[:, cols],
                        start=True,
                        stop=False,
                    )
                    nc.tensor.matmul_mx(
                        out=ps[:, t, :],
                        lhsT=wp_q[e][0][:, ch].bitcast(FP8X4),
                        lhsT_scale=wp_q[e][1][:, ch],
                        rhs=par_w[:, cols].bitcast(FP8X4),
                        rhs_scale=par_s[:, cols],
                        start=False,
                        stop=True,
                    )
                h_ps[e, h] = ps

        def round_h(e):
            if e == 0:
                first = keep.tile([P, 2, C, PACK], BF16, name="h_bf01", tag=f"stage{E - 1}", align_bytes=64)
                h_bf[0], h_bf[1] = first[:, 0], first[:, 1]
            if e > 1:
                h_bf[e] = ring.tile([P, C, PACK], BF16, name="h_bf", align_bytes=64)
            t = h_bf[e]
            for h in range(2):
                cp = nc.vector.tensor_copy if (e == E - 1 and h == 1) else nc.scalar.copy
                cp(out=t[:, h * HALF : (h + 1) * HALF, :], in_=h_ps[e, h][:].rearrange("p t n -> p n t"))

        def quant_h(e):
            w = ring.tile([P, C], U32, name="h_w", align_bytes=64)
            s = ring.tile([P, C], U8, name="h_s", align_bytes=64)
            nc.vector.quantize_mx(out=w[:].bitcast(FP8X4), scales=s[:], in_=h_bf[e][:].rearrange("p n t -> p (n t)"))
            h_q[e] = (w, s)

        def last_expert(e):
            banks = []
            for h in range(2):
                cols = slice(h * HALF, (h + 1) * HALF)
                ps = psum.tile([P, PACK, HALF], F32, name="y_ps")
                for t in range(PACK):
                    nc.tensor.matmul_mx(
                        out=ps[:, t, :],
                        lhsT=w_dealt[1, e][:, t, :].bitcast(FP8X4),
                        lhsT_scale=plane(1, e)[:, t * P : (t + 1) * P],
                        rhs=h_q[e][0][:, cols].bitcast(FP8X4),
                        rhs_scale=h_q[e][1][:, cols],
                        start=True,
                        stop=True,
                    )
                banks.append(ps)
            yb = ring.tile([P, C, PACK], BF16, name="y_bf", align_bytes=64)
            for h in range(2):
                cols = slice(h * HALF, (h + 1) * HALF)
                yf = keep.tile([P, PACK, HALF], F32, name=f"y_f{e}_{h}")
                nc.scalar.copy(out=yf[:], in_=banks[h][:])
                nc.sync.dma_start(
                    out=out_0.rearrange("(p t) j -> p t j", t=PACK)[:, :, e * C + h * HALF : e * C + (h + 1) * HALF],
                    in_=yf[:],
                )
                nc.vector.tensor_copy(
                    out=yb[:, cols, :].rearrange("p (c i) t -> p c t i", i=4),
                    in_=yf[:].rearrange("p t (c i) -> p c t i", i=4),
                )
            y_bf[e] = yb

        def layer2(e):
            for b in range(2):
                ps = psum.tile([P, 2, C], F32, name="y_ps")
                for i in range(2):
                    t = 2 * b + i
                    nc.tensor.matmul_mx(
                        out=ps[:, i, :],
                        lhsT=w_dealt[1, e][:, t, :].bitcast(FP8X4),
                        lhsT_scale=plane(1, e)[:, t * P : (t + 1) * P],
                        rhs=h_q[e][0][:].bitcast(FP8X4),
                        rhs_scale=h_q[e][1][:],
                        start=True,
                        stop=True,
                    )
                y_ps[e, b] = ps

        def copy_y(e):
            t = keep.tile([P, PACK, C], F32, name=f"y_f{e}")
            for b in range(2):
                nc.scalar.copy(out=t[:, 2 * b : 2 * b + 2, :], in_=y_ps[e, b][:])
            y_f[e] = t
            nc.sync.dma_start(out=out_0.rearrange("(p t) j -> p t j", t=PACK)[:, :, e * C : (e + 1) * C], in_=t[:])

        def round_y(e):
            t = ring.tile([P, C, PACK], BF16, name="y_bf", align_bytes=64)
            nc.vector.tensor_copy(
                out=t[:].rearrange("p (c i) t -> p c t i", i=4), in_=y_f[e][:].rearrange("p t (c i) -> p c t i", i=4)
            )
            y_bf[e] = t

        def quant_y(e):
            if e % 2 == 0:
                y_pair[1] = keep.tile([P, 2 * C], U32, name=f"y_w{e}", align_bytes=64)
            w = y_pair[1]
            nc.vector.quantize_mx(
                out=w[:, (e % 2) * C : (e % 2 + 1) * C].bitcast(FP8X4),
                scales=y_s[:, e * C : (e + 1) * C],
                in_=y_bf[e][:].rearrange("p n t -> p (n t)"),
            )
            if e % 2 == 1:
                nc.sync.dma_start(
                    out=out_1[0].rearrange("p n t -> p (n t)").bitcast(I32)[:, (e - 1) * C : (e + 1) * C], in_=w[:].bitcast(I32)
                )

        gather(x_w[:].bitcast(U32), U32, "w")
        gather(x_s[:], U8, "s")
        for e in range(E):
            round_wp(e)
        for g in range(3):
            deal_scales(g)
        for e in range(E + 2):
            if e < E:
                quant_wp(e)
                deal_words(0, e)
                layer1(e)
                round_h(e)
                deal_words(1, e)
            if 1 <= e <= E:
                quant_h(e - 1)
                if e < E:
                    layer2(e - 1)
                    copy_y(e - 1)
                else:
                    last_expert(e - 1)
            if e >= 2:
                if e - 2 < E - 1:
                    round_y(e - 2)
                quant_y(e - 2)
        for q in range(QUADS):
            nc.sync.dma_start(
                out=out_2.bitcast(I32)[0, 4 * q : 4 * q + 4, :], in_=y_s[:].bitcast(I32)[32 * q : 32 * q + 4, :]
            )
